import numpy as np
import ml_dtypes


def mxq(x, axis, fmt="e4m3"):
    dtype, down = {"e4m3": (ml_dtypes.float8_e4m3fn, 7), "e5m2": (ml_dtypes.float8_e5m2, 14)}[fmt]
    v = np.moveaxis(np.asarray(x, np.float32).astype(ml_dtypes.bfloat16).astype(np.float64), axis, -1)
    blocks = v.reshape(v.shape[:-1] + (-1, 32))
    amax = np.abs(blocks).max(-1, keepdims=True)
    byte = np.maximum(np.where(amax > 0, np.frexp(amax)[1] - 1 + 127, 0) - down, 1)
    scale = np.exp2(byte - 127.0)
    codes = (blocks / scale).astype(np.float32).astype(dtype).astype(np.float64)
    return np.moveaxis((codes * scale).reshape(v.shape), -1, axis)


WIDE = False


def mx_kscale(k):
    if not WIDE:
        return np.ones(k)
    levels = np.array([10, -10, 5, -5, 0])
    if k % 512:
        return np.exp2(np.random.permutation(np.resize(levels, k // 32))).repeat(32)
    a = np.empty((k // 512, 16))
    for p in range(k // 512):
        a[p, :8] = np.random.permutation(np.resize(levels, 8))
        for g in range(8):
            far = levels[np.abs(levels - a[p, g]) >= 10]
            a[p, g + 8] = far[np.random.randint(len(far))]
    return np.exp2(a.ravel()).repeat(32)


def f64(x):
    return np.asarray(x).astype(np.float64)


def striped(idx):
    return np.tile(idx.reshape(-1, 16).T, (8, 1)).astype(np.uint16)


def unstriped(offs):
    return offs[:16].T.reshape(-1).astype(np.int64)


def pack_weight(w):
    k, n = w.shape
    w = f64(np.asarray(w, np.float32).astype(ml_dtypes.bfloat16)).reshape(k // 32, 32, n)
    amax = np.abs(w).max(1)
    byte = np.clip(np.where(amax > 0, np.frexp(amax)[1] - 1 + 127 - 7, 1), 1, 254)
    scaled = (w * np.exp2(127.0 - byte)[:, None, :]).reshape(k, n).astype(np.float32)
    words = np.ascontiguousarray(scaled.reshape(k // 512, 128, 4, n).transpose(0, 1, 3, 2)).astype(ml_dtypes.float8_e4m3fn).view(np.uint8)
    return words, np.ascontiguousarray(byte.astype(np.uint8).reshape(k // 512, 16, n))


def unpack_weight(words, scales):
    g, p, n, _ = words.shape
    vals = np.ascontiguousarray(words).view(ml_dtypes.float8_e4m3fn).astype(np.float64) * np.repeat(np.exp2(scales.astype(np.float64) - 127.0), 8, axis=1)[..., None]
    return vals.transpose(0, 1, 3, 2).reshape(g * 512, n)


E2M1 = np.array([0.0, 0.5, 1.0, 1.5, 2.0, 3.0, 4.0, 6.0, -0.0, -0.5, -1.0, -1.5, -2.0, -3.0, -4.0, -6.0])


def pack_fp4(w):
    k, n = w.shape
    w = f64(np.asarray(w, np.float32).astype(ml_dtypes.bfloat16)).reshape(k // 32, 32, n)
    amax = np.abs(w).max(1)
    mant, ex = np.frexp(amax / 6.0)
    byte = np.clip(np.where(amax > 0, np.where(mant > 0.5, ex, ex - 1) + 127, 1), 1, 254)
    scaled = (w * np.exp2(127.0 - byte)[:, None, :]).reshape(k, n).astype(np.float32)
    c = np.ascontiguousarray(scaled.reshape(k // 512, 128, 4, n).transpose(0, 1, 3, 2)).astype(ml_dtypes.float4_e2m1fn).view(np.uint8) & 0xF
    words = (c[..., 0::2] | (c[..., 1::2] << 4)).reshape(k // 512, 128, 2 * n)
    return np.ascontiguousarray(words), np.ascontiguousarray(byte.astype(np.uint8).reshape(k // 512, 16, n))


def unpack_fp4(words, scales):
    g, _, n = scales.shape
    words = np.ascontiguousarray(words).reshape(g, 128, n, 2)
    nib = np.empty((g, 128, n, 4), np.uint8)
    nib[..., 0::2] = words & 0xF
    nib[..., 1::2] = words >> 4
    vals = E2M1[nib] * np.repeat(np.exp2(scales.astype(np.float64) - 127.0), 8, axis=1)[..., None]
    return vals.transpose(0, 1, 3, 2).reshape(g * 512, n)


def relu(v):
    return np.maximum(v, 0.0)


K, T, S, D, N, H, U = 1024, 2048, 1024, 4, 128, 512, 512


def setup_inputs():
    n = np.random.standard_normal
    s = mx_kscale(K)[:, None]
    u = mx_kscale(H)
    packed_xT = pack_weight(n((K, T)) * s)
    packed_w1 = pack_fp4(n((K, H)) / np.sqrt(K) / s)
    packed_w2 = pack_fp4(n((H, N)) / np.sqrt(H) / u[:, None])
    return {
        "x_words": packed_xT[0],
        "x_scales": packed_xT[1],
        "w1_words": packed_w1[0],
        "w1_scales": packed_w1[1],
        "flr": (np.random.uniform(-0.6, 0.3, (H, U))).astype(np.float32),
        "unit": (np.random.uniform(0.6, 1.4, (H, 1)) * u[:, None]).astype(np.float32),
        "w2_words": packed_w2[0],
        "w2_scales": packed_w2[1],
        "offs": striped(np.random.permutation(T)[:S]),
        "got": striped(np.random.permutation(S)[:U]),
    }


def reference(x_words, x_scales, w1_words, w1_scales, flr, unit, w2_words, w2_scales, offs, got):
    xq = unpack_weight(x_words, x_scales)[:, unstriped(offs)]
    y = unpack_fp4(w1_words, w1_scales).T @ xq
    sg = y[:, unstriped(got)]
    sc = np.maximum(sg, f64(flr))
    sum4 = sc.reshape(len(sc), -1, D).sum(axis=2)
    dv = sc - (0.25 * np.repeat(sum4, D, axis=1))
    hid = f64(unit) * (dv * relu(sc))
    return unpack_fp4(w2_words, w2_scales).T @ mxq(hid, 0, "e4m3")

@@ -1,0 +1,272 @@
+from contextlib import ExitStack
+
+import concourse.mybir as mybir
+
+K, T, S, D, N, H, U = 1024, 2048, 1024, 4, 128, 512, 512
+FLOPS = 2 * K * H * S + 2 * H * N * U
+
+F32 = mybir.dt.float32
+BF16 = mybir.dt.bfloat16
+I32 = mybir.dt.int32
+U32 = mybir.dt.uint32
+U16 = mybir.dt.uint16
+U8 = mybir.dt.uint8
+FP8X4 = mybir.dt.float8_e4m3fn_x4
+FP4X4 = mybir.dt.float4_e2m1fn_x4
+ALU = mybir.AluOpType
+COPY = mybir.ActivationFunctionType.Copy
+
+P = 128
+PACK = 4
+PASSES = K // (P * PACK)
+HALF = 512
+HALVES = S // HALF
+PER_COL = 16
+CHUNKS = ((0, 256), (256, 128), (384, 128))
+XS_AT = 8192
+VECTOR_EVAC = ((0, 1), (1, 1), (2, 1))
+
+
+def tile_picked_yxtrim_rect_p_kernel(
+    tc, x_words, x_scales, w1_words, w1_scales, flr, unit, w2_words, w2_scales, offs, got, out
+):
+    nc = tc.nc
+    with ExitStack() as ctx:
+        lists = ctx.enter_context(tc.tile_pool(name="lists", bufs=1))
+        keep = ctx.enter_context(tc.tile_pool(name="keep", bufs=1))
+        shared = ctx.enter_context(tc.tile_pool(name="shared", bufs=1))
+        psum = ctx.enter_context(tc.psum_pool(name="psum", bufs=1))
+
+        offs_sb = lists.tile([P, S // PER_COL], U16, name="offs_sb")
+        got_sb = lists.tile([P, U // PER_COL], U16, name="got_sb")
+        nc.sync.dma_start(offs_sb[:], offs)
+        nc.sync.dma_start(got_sb[:], got)
+
+        xs_table = shared.tile([P, T], U8, name="xs_table", align_bytes=64, offset=XS_AT)
+        nc.vector.memset(xs_table[:].bitcast(I32), 0)
+        w1s_raw = keep.tile([P, PASSES, H], U8, name="w1s_raw", align_bytes=64)
+        nc.gpsimd.memset(w1s_raw[:].bitcast(I32), 0)
+
+        w1_raw = keep.tile([P, PASSES, 2 * H], U8, name="w1_raw", tag="w1_then_x1", align_bytes=64)
+        nc.sync.dma_start(w1_raw[:].bitcast(I32), w1_words.rearrange("o p c -> p o c").bitcast(I32))
+
+        xs_rows = x_scales.rearrange("o (q j) c -> j q o c", j=4)
+        for j in range(4):
+            nc.scalar.dma_start(xs_table[j:P:16, :].bitcast(I32), xs_rows[j].bitcast(I32))
+
+        def load_words(o, tag):
+            table = keep.tile([P, T], I32, name="xw_table%d" % o, tag=tag, align_bytes=64)
+            nc.sync.dma_start(table[:], x_words[o].rearrange("p n t -> p (n t)").bitcast(I32))
+            return table
+
+        xw_table = [load_words(0, "x0")]
+
+        w1s_rows = w1_scales.rearrange("o (q j) c -> j q o c", j=4)
+        for j in range(4):
+            nc.gpsimd.dma_start(w1s_raw[j:P:32, :, :].bitcast(I32), w1s_rows[j].bitcast(I32))
+
+        w1_cols = w1_raw[:].rearrange("p o (m t b) -> p t o m b", t=PACK, b=2)
+        w1s_cols = w1s_raw[:].rearrange("p o (m t) -> p t o m", t=PACK)
+        w1_dealt = [keep.tile([P, PASSES, 2 * P], U8, name="w1_dealt%d" % t, align_bytes=64) for t in range(PACK)]
+        w1s_dealt = [
+            shared.tile([P, PASSES, P], U8, name="w1s_dealt%d" % t, align_bytes=64, offset=XS_AT + 512 + 256 * t)
+            for t in range(PACK)
+        ]
+
+        for t in range(PACK):
+            nc.vector.tensor_copy(w1_dealt[t][:].rearrange("p o (m b) -> p o m b", b=2), w1_cols[:, t])
+        xw_table.append(load_words(1, "w1_then_x1"))
+
+        xs_pass1 = keep.tile([P, S], U8, name="xs_pass1", align_bytes=64)
+        nc.gpsimd.memset(xs_pass1[96:P, :].bitcast(I32), 0)
+        xs_picked = keep.tile([P, S], U8, name="xs_picked", align_bytes=64)
+        nc.vector.tensor_copy(xs_picked[:], xs_table[:].indirect(offs_sb[:]))
+        nc.scalar.dma_start(xs_pass1[0 : P - 16, :].bitcast(I32), xs_picked[16:P, :].bitcast(I32))
+        xs_planes = (xs_picked, xs_pass1)
+
+        flr_sb = shared.tile([P, PACK, U], F32, name="flr_sb", offset=64)
+        nc.sync.dma_start(flr_sb[:], flr.rearrange("(p t) r -> p t r", t=PACK))
+        unit_sb = shared.tile([P, PACK], F32, name="unit_sb", offset=XS_AT + 64)
+        nc.sync.dma_start(unit_sb[:], unit.rearrange("(p t) o -> p (t o)", t=PACK))
+        w2_sb = shared.tile([P, 2 * N], U8, name="w2_sb", align_bytes=64, offset=XS_AT + 128)
+        nc.sync.dma_start(w2_sb[:].bitcast(I32), w2_words[0].bitcast(I32))
+        w2s_sb = shared.tile([P, N], U8, name="w2s_sb", align_bytes=64, offset=XS_AT + 384)
+        nc.gpsimd.memset(w2s_sb[:].bitcast(I32), 0)
+        for q in range(4):
+            nc.sync.dma_start(
+                w2s_sb[32 * q : 32 * q + 4, :].bitcast(I32), w2_scales[0, 4 * q : 4 * q + 4, :].bitcast(I32)
+            )
+
+        xw_picked = [
+            shared.tile([P, S], U32, name="xw_picked0", align_bytes=64, offset=XS_AT + 1536),
+            keep.tile([P, S], U32, name="xw_picked1", align_bytes=64),
+        ]
+
+        def pick(o, h):
+            cols = slice(h * HALF // PER_COL, (h + 1) * HALF // PER_COL)
+            nc.vector.tensor_copy(
+                xw_picked[o][:, h * HALF : (h + 1) * HALF], xw_table[o][:].bitcast(U32).indirect(offs_sb[:, cols])
+            )
+
+        banks = {}
+        for t in range(PACK):
+            for h in range(HALVES):
+                banks[t, h] = psum.tile([P, HALF], F32, name="bank%d_%d" % (t, h), tag="bank%d_%d" % (t, h))
+        y = [keep.tile([P, S], F32, name="y%d" % t, align_bytes=64) for t in range(PACK)]
+
+        def first_product(o, h, t):
+            nc.tensor.matmul_mx(
+                out=banks[t, h][:],
+                lhsT=w1_dealt[t][:, o, :].bitcast(FP4X4),
+                lhsT_scale=w1s_dealt[t][:, o, :],
+                rhs=xw_picked[o][:, h * HALF : (h + 1) * HALF].bitcast(FP8X4),
+                rhs_scale=xs_planes[o][:, h * HALF : (h + 1) * HALF],
+                start=(o == 0),
+                stop=(o == PASSES - 1),
+            )
+
+        def evacuate(t, h):
+            cols = slice(h * HALF, (h + 1) * HALF)
+            if (t, h) in VECTOR_EVAC:
+                nc.vector.tensor_copy(y[t][:, cols], banks[t, h][:])
+            else:
+                nc.scalar.copy(y[t][:, cols], banks[t, h][:])
+
+        pick(0, 0)
+        for t in range(PACK):
+            nc.vector.tensor_copy(w1s_dealt[t][:], w1s_cols[:, t])
+        for o in range(PASSES):
+            for h in range(HALVES):
+                if (o, h) != (0, 0):
+                    pick(o, h)
+                for t in range(PACK):
+                    first_product(o, h, t)
+
+        work = {}
+        for c, (r0, w) in enumerate(CHUNKS):
+            work[c] = dict(
+                sg=keep.tile([P, PACK, w], F32, name="sg%d" % c),
+                sc=keep.tile([P, PACK, w], F32, name="sc%d" % c),
+                pair=keep.tile([P, PACK * w // D, 2], F32, name="pair%d" % c),
+                sum4=keep.tile([P, PACK * w // D], F32, name="sum4_%d" % c),
+                dv=keep.tile([P, PACK, w], F32, name="dv%d" % c),
+                ru=keep.tile([P, PACK, w], F32, name="ru%d" % c),
+                hid=keep.tile([P, w * PACK], BF16, name="hid%d" % c, align_bytes=64),
+                codes=keep.tile([P, w], U32, name="codes%d" % c, align_bytes=64),
+                scales=keep.tile([P, w], U8, name="scales%d" % c, align_bytes=64),
+                res=keep.tile([P, w], F32, name="res%d" % c),
+            )
+
+        def fetch(c, t):
+            r0, w = CHUNKS[c]
+            cols = slice(r0 // PER_COL, (r0 + w) // PER_COL)
+            nc.scalar.activation(work[c]["sg"][:, t, :], y[t][:].indirect(got_sb[:, cols]), COPY)
+
+        def groups(c, name, t0, t1):
+            return work[c][name][:, t0:t1, :].rearrange("p t (j d) -> p (t j) d", d=D)
+
+        def floor_step(c, t0, t1):
+            r0, w = CHUNKS[c]
+            nc.vector.tensor_tensor(
+                work[c]["sc"][:, t0:t1, :], work[c]["sg"][:, t0:t1, :], flr_sb[:, t0:t1, r0 : r0 + w], ALU.max
+            )
+
+        def pair_step(c, t0, t1):
+            g = CHUNKS[c][1] // D
+            sc = groups(c, "sc", t0, t1)
+            nc.vector.tensor_tensor(work[c]["pair"][:, t0 * g : t1 * g, :], sc[:, :, 0:2], sc[:, :, 2:4], ALU.add)
+
+        def sum_step(c, t0, t1):
+            g = CHUNKS[c][1] // D
+            pair = work[c]["pair"][:, t0 * g : t1 * g, :]
+            nc.vector.tensor_tensor(work[c]["sum4"][:, t0 * g : t1 * g], pair[:, :, 0], pair[:, :, 1], ALU.add)
+
+        def centre_step(c, t0, t1):
+            g = CHUNKS[c][1] // D
+            sums = work[c]["sum4"][:, t0 * g : t1 * g].unsqueeze(2).to_broadcast([P, (t1 - t0) * g, D])
+            nc.vector.scalar_tensor_tensor(
+                groups(c, "dv", t0, t1), sums, -1.0 / D, groups(c, "sc", t0, t1), ALU.mult, ALU.add
+            )
+
+        def relu_step(c, t):
+            nc.vector.tensor_scalar(
+                work[c]["ru"][:, t, :], work[c]["sc"][:, t, :], 0.0, unit_sb[:, t : t + 1], ALU.max, ALU.mult
+            )
+
+        def hidden_step(c):
+            nc.vector.tensor_tensor(
+                work[c]["hid"][:].rearrange("p (c i t) -> p c t i", i=2, t=PACK),
+                work[c]["dv"][:].rearrange("p t (c i) -> p c t i", i=2),
+                work[c]["ru"][:].rearrange("p t (c i) -> p c t i", i=2),
+                ALU.mult,
+            )
+
+        def quantise(c):
+            nc.vector.quantize_mx(
+                out=work[c]["codes"][:].bitcast(FP8X4), scales=work[c]["scales"][:], in_=work[c]["hid"][:]
+            )
+
+        def second_product(c):
+            r0, w = CHUNKS[c]
+            acc = psum.tile([P, w], F32, name="acc%d" % c, tag="bank%d_0" % c)
+            nc.tensor.matmul_mx(
+                out=acc[:],
+                lhsT=w2_sb[:].bitcast(FP4X4),
+                lhsT_scale=w2s_sb[:],
+                rhs=work[c]["codes"][:].bitcast(FP8X4),
+                rhs_scale=work[c]["scales"][:],
+                start=True,
+                stop=True,
+            )
+            nc.scalar.copy(work[c]["res"][:], acc[:])
+            nc.sync.dma_start(out[:, r0 : r0 + w], work[c]["res"][:])
+
+        evacuate(0, 0)
+        evacuate(1, 0)
+        evacuate(0, 1)
+        evacuate(2, 0)
+        evacuate(1, 1)
+        fetch(0, 0)
+        fetch(0, 1)
+        evacuate(2, 1)
+        evacuate(3, 0)
+        evacuate(3, 1)
+        fetch(0, 2)
+        fetch(0, 3)
+        for c in range(1, len(CHUNKS)):
+            for t in range(PACK):
+                fetch(c, t)
+
+        floor_step(0, 0, 2)
+        relu_step(0, 0)
+        pair_step(0, 0, 2)
+        relu_step(0, 1)
+        sum_step(0, 0, 2)
+        floor_step(0, 2, 4)
+        centre_step(0, 0, 2)
+        pair_step(0, 2, 4)
+        relu_step(0, 2)
+        sum_step(0, 2, 4)
+        relu_step(0, 3)
+        centre_step(0, 2, 4)
+        floor_step(1, 0, 4)
+        hidden_step(0)
+        pair_step(1, 0, 4)
+        quantise(0)
+        second_product(0)
+        sum_step(1, 0, 4)
+        floor_step(2, 0, 4)
+        centre_step(1, 0, 4)
+        pair_step(2, 0, 4)
+        for t in range(PACK):
+            relu_step(1, t)
+        sum_step(2, 0, 4)
+        hidden_step(1)
+        centre_step(2, 0, 4)
+        quantise(1)
+        second_product(1)
+        for t in range(PACK):
+            relu_step(2, t)
+        hidden_step(2)
+        quantise(2)
+        second_product(2)

@@ -15,6 +15,7 @@ FP8X4 = mybir.dt.float8_e4m3fn_x4
 FP4X4 = mybir.dt.float4_e2m1fn_x4
 ALU = mybir.AluOpType
 COPY = mybir.ActivationFunctionType.Copy
+RELU = mybir.ActivationFunctionType.Relu
 
 P = 128
 PACK = 4
@@ -22,9 +23,9 @@ PASSES = K // (P * PACK)
 HALF = 512
 HALVES = S // HALF
 PER_COL = 16
-CHUNKS = ((0, 256), (256, 128), (384, 128))
-XS_AT = 8192
-VECTOR_EVAC = ((0, 1), (1, 1), (2, 1))
+PIECES = ((0, 256), (256, 128), (384, 128))
+W1S_AT = 8192
+XS_AT = W1S_AT + 1024
 
 
 def tile_picked_yxtrim_rect_p_kernel(
@@ -37,22 +38,23 @@ def tile_picked_yxtrim_rect_p_kernel(
         shared = ctx.enter_context(tc.tile_pool(name="shared", bufs=1))
         psum = ctx.enter_context(tc.psum_pool(name="psum", bufs=1))
 
+        xs_table = shared.tile([P, T], U8, name="xs_table", align_bytes=64, offset=XS_AT)
+        nc.gpsimd.memset(xs_table[:, T // 4 : T].bitcast(I32), 0)
+        nc.vector.memset(xs_table[:, 0 : T // 4].bitcast(I32), 0)
+        w1s_raw = shared.tile([P, PASSES, H], U8, name="w1s_raw", align_bytes=64, offset=W1S_AT)
+        nc.vector.memset(w1s_raw[:].bitcast(I32), 0)
+
         offs_sb = lists.tile([P, S // PER_COL], U16, name="offs_sb")
         got_sb = lists.tile([P, U // PER_COL], U16, name="got_sb")
         nc.sync.dma_start(offs_sb[:], offs)
         nc.sync.dma_start(got_sb[:], got)
-
-        xs_table = shared.tile([P, T], U8, name="xs_table", align_bytes=64, offset=XS_AT)
-        nc.vector.memset(xs_table[:].bitcast(I32), 0)
-        w1s_raw = keep.tile([P, PASSES, H], U8, name="w1s_raw", align_bytes=64)
-        nc.gpsimd.memset(w1s_raw[:].bitcast(I32), 0)
 
         w1_raw = keep.tile([P, PASSES, 2 * H], U8, name="w1_raw", tag="w1_then_x1", align_bytes=64)
         nc.sync.dma_start(w1_raw[:].bitcast(I32), w1_words.rearrange("o p c -> p o c").bitcast(I32))
 
         xs_rows = x_scales.rearrange("o (q j) c -> j q o c", j=4)
         for j in range(4):
-            nc.scalar.dma_start(xs_table[j:P:16, :].bitcast(I32), xs_rows[j].bitcast(I32))
+            nc.sync.dma_start(xs_table[j:P:16, :].bitcast(I32), xs_rows[j].bitcast(I32))
 
         def load_words(o, tag):
             table = keep.tile([P, T], I32, name="xw_table%d" % o, tag=tag, align_bytes=64)
@@ -63,42 +65,27 @@ def tile_picked_yxtrim_rect_p_kernel(
 
         w1s_rows = w1_scales.rearrange("o (q j) c -> j q o c", j=4)
         for j in range(4):
-            nc.gpsimd.dma_start(w1s_raw[j:P:32, :, :].bitcast(I32), w1s_rows[j].bitcast(I32))
+            nc.scalar.dma_start(w1s_raw[j:P:32, :, :].bitcast(I32), w1s_rows[j].bitcast(I32))
 
-        w1_cols = w1_raw[:].rearrange("p o (m t b) -> p t o m b", t=PACK, b=2)
-        w1s_cols = w1s_raw[:].rearrange("p o (m t) -> p t o m", t=PACK)
-        w1_dealt = [keep.tile([P, PASSES, 2 * P], U8, name="w1_dealt%d" % t, align_bytes=64) for t in range(PACK)]
-        w1s_dealt = [
-            shared.tile([P, PASSES, P], U8, name="w1s_dealt%d" % t, align_bytes=64, offset=XS_AT + 512 + 256 * t)
-            for t in range(PACK)
-        ]
-
-        for t in range(PACK):
-            nc.vector.tensor_copy(w1_dealt[t][:].rearrange("p o (m b) -> p o m b", b=2), w1_cols[:, t])
+        w1_dealt = keep.tile([P, PASSES, PACK, 2 * P], U8, name="w1_dealt", align_bytes=64)
+        w1s_dealt = shared.tile([P, PASSES, PACK, P], U8, name="w1s_dealt", align_bytes=64, offset=XS_AT)
+        nc.vector.tensor_copy(
+            w1_dealt[:].bitcast(U16), w1_raw[:].bitcast(U16).rearrange("p o (m t) -> p o t m", t=PACK)
+        )
         xw_table.append(load_words(1, "w1_then_x1"))
 
         xs_pass1 = keep.tile([P, S], U8, name="xs_pass1", align_bytes=64)
-        nc.gpsimd.memset(xs_pass1[96:P, :].bitcast(I32), 0)
+        nc.gpsimd.memset(xs_pass1[:].bitcast(I32), 0)
         xs_picked = keep.tile([P, S], U8, name="xs_picked", align_bytes=64)
         nc.vector.tensor_copy(xs_picked[:], xs_table[:].indirect(offs_sb[:]))
-        nc.scalar.dma_start(xs_pass1[0 : P - 16, :].bitcast(I32), xs_picked[16:P, :].bitcast(I32))
+        for q in range(4):
+            nc.scalar.dma_start(
+                xs_pass1[32 * q : 32 * q + 4, :].bitcast(I32), xs_picked[32 * q + 16 : 32 * q + 20, :].bitcast(I32)
+            )
         xs_planes = (xs_picked, xs_pass1)
 
-        flr_sb = shared.tile([P, PACK, U], F32, name="flr_sb", offset=64)
-        nc.sync.dma_start(flr_sb[:], flr.rearrange("(p t) r -> p t r", t=PACK))
-        unit_sb = shared.tile([P, PACK], F32, name="unit_sb", offset=XS_AT + 64)
-        nc.sync.dma_start(unit_sb[:], unit.rearrange("(p t) o -> p (t o)", t=PACK))
-        w2_sb = shared.tile([P, 2 * N], U8, name="w2_sb", align_bytes=64, offset=XS_AT + 128)
-        nc.sync.dma_start(w2_sb[:].bitcast(I32), w2_words[0].bitcast(I32))
-        w2s_sb = shared.tile([P, N], U8, name="w2s_sb", align_bytes=64, offset=XS_AT + 384)
-        nc.gpsimd.memset(w2s_sb[:].bitcast(I32), 0)
-        for q in range(4):
-            nc.sync.dma_start(
-                w2s_sb[32 * q : 32 * q + 4, :].bitcast(I32), w2_scales[0, 4 * q : 4 * q + 4, :].bitcast(I32)
-            )
-
         xw_picked = [
-            shared.tile([P, S], U32, name="xw_picked0", align_bytes=64, offset=XS_AT + 1536),
+            shared.tile([P, S], U32, name="xw_picked0", align_bytes=64, offset=XS_AT + 1024),
             keep.tile([P, S], U32, name="xw_picked1", align_bytes=64),
         ]
 
@@ -108,165 +95,151 @@ def tile_picked_yxtrim_rect_p_kernel(
                 xw_picked[o][:, h * HALF : (h + 1) * HALF], xw_table[o][:].bitcast(U32).indirect(offs_sb[:, cols])
             )
 
-        banks = {}
-        for t in range(PACK):
-            for h in range(HALVES):
-                banks[t, h] = psum.tile([P, HALF], F32, name="bank%d_%d" % (t, h), tag="bank%d_%d" % (t, h))
         y = [keep.tile([P, S], F32, name="y%d" % t, align_bytes=64) for t in range(PACK)]
+        banks = {}
 
-        def first_product(o, h, t):
+        def first_product(o, t, h, bank):
+            cols = slice(h * HALF, (h + 1) * HALF)
+            if o == 0:
+                banks[t, h] = psum.tile([P, HALF], F32, name="acc%d_%d" % (t, h), tag="bank%d" % bank)
             nc.tensor.matmul_mx(
                 out=banks[t, h][:],
-                lhsT=w1_dealt[t][:, o, :].bitcast(FP4X4),
-                lhsT_scale=w1s_dealt[t][:, o, :],
-                rhs=xw_picked[o][:, h * HALF : (h + 1) * HALF].bitcast(FP8X4),
-                rhs_scale=xs_planes[o][:, h * HALF : (h + 1) * HALF],
+                lhsT=w1_dealt[:, o, t, :].bitcast(FP4X4),
+                lhsT_scale=w1s_dealt[:, o, t, :],
+                rhs=xw_picked[o][:, cols].bitcast(FP8X4),
+                rhs_scale=xs_planes[o][:, cols],
                 start=(o == 0),
                 stop=(o == PASSES - 1),
             )
 
-        def evacuate(t, h):
-            cols = slice(h * HALF, (h + 1) * HALF)
-            if (t, h) in VECTOR_EVAC:
-                nc.vector.tensor_copy(y[t][:, cols], banks[t, h][:])
-            else:
-                nc.scalar.copy(y[t][:, cols], banks[t, h][:])
+        def empty_on_scalar(t, h):
+            nc.scalar.copy(y[t][:, h * HALF : (h + 1) * HALF], banks[t, h][:])
 
+        def empty_on_vector(t, h):
+            nc.vector.tensor_copy(y[t][:, h * HALF : (h + 1) * HALF], banks[t, h][:])
+
+        last = PACK - 1
         pick(0, 0)
-        for t in range(PACK):
-            nc.vector.tensor_copy(w1s_dealt[t][:], w1s_cols[:, t])
+        nc.vector.tensor_copy(w1s_dealt[:], w1s_raw[:].rearrange("p o (m t) -> p o t m", t=PACK))
+
+        flr_sb = shared.tile([P, PACK, U], F32, name="flr_sb", offset=64)
+        nc.sync.dma_start(flr_sb[:], flr.rearrange("(p t) r -> p t r", t=PACK))
+        unit_sb = shared.tile([P, PACK], F32, name="unit_sb", offset=W1S_AT + 64)
+        nc.sync.dma_start(unit_sb[:], unit.rearrange("(p t) o -> p (t o)", t=PACK))
+        w2_sb = shared.tile([P, 2 * N], U8, name="w2_sb", align_bytes=64, offset=W1S_AT + 128)
+        nc.sync.dma_start(w2_sb[:].bitcast(I32), w2_words[0].bitcast(I32))
+        w2s_sb = shared.tile([P, N], U8, name="w2s_sb", align_bytes=64, offset=W1S_AT + 384)
+        nc.gpsimd.memset(w2s_sb[:].bitcast(I32), 0)
+        for q in range(4):
+            nc.sync.dma_start(
+                w2s_sb[32 * q : 32 * q + 4, :].bitcast(I32), w2_scales[0, 4 * q : 4 * q + 4, :].bitcast(I32)
+            )
+
         for o in range(PASSES):
             for h in range(HALVES):
                 if (o, h) != (0, 0):
                     pick(o, h)
-                for t in range(PACK):
-                    first_product(o, h, t)
+                for t in range(last):
+                    first_product(o, t, h, HALVES * t + h)
 
-        work = {}
-        for c, (r0, w) in enumerate(CHUNKS):
-            work[c] = dict(
-                sg=keep.tile([P, PACK, w], F32, name="sg%d" % c),
-                sc=keep.tile([P, PACK, w], F32, name="sc%d" % c),
-                pair=keep.tile([P, PACK * w // D, 2], F32, name="pair%d" % c),
-                sum4=keep.tile([P, PACK * w // D], F32, name="sum4_%d" % c),
-                dv=keep.tile([P, PACK, w], F32, name="dv%d" % c),
-                ru=keep.tile([P, PACK, w], F32, name="ru%d" % c),
-                hid=keep.tile([P, w * PACK], BF16, name="hid%d" % c, align_bytes=64),
-                codes=keep.tile([P, w], U32, name="codes%d" % c, align_bytes=64),
-                scales=keep.tile([P, w], U8, name="scales%d" % c, align_bytes=64),
-                res=keep.tile([P, w], F32, name="res%d" % c),
-            )
+        sg = [keep.tile([P, U], F32, name="sg%d" % t) for t in range(PACK)]
+        sc = [keep.tile([P, U], F32, name="sc%d" % t) for t in range(PACK)]
+        pair = [keep.tile([P, U // D, 2], F32, name="pair%d" % t) for t in range(PACK)]
+        sum4 = [keep.tile([P, U // D], F32, name="sum4_%d" % t) for t in range(PACK)]
+        dv = keep.tile([P, PACK, U], F32, name="dv")
+        ru = keep.tile([P, PACK, U], F32, name="ru")
 
-        def fetch(c, t):
-            r0, w = CHUNKS[c]
-            cols = slice(r0 // PER_COL, (r0 + w) // PER_COL)
-            nc.scalar.activation(work[c]["sg"][:, t, :], y[t][:].indirect(got_sb[:, cols]), COPY)
+        def floor_step(t, r0=0, r1=U):
+            nc.vector.tensor_tensor(sc[t][:, r0:r1], sg[t][:, r0:r1], flr_sb[:, t, r0:r1], ALU.max)
 
-        def groups(c, name, t0, t1):
-            return work[c][name][:, t0:t1, :].rearrange("p t (j d) -> p (t j) d", d=D)
+        def pair_step(t):
+            groups = sc[t][:, :].rearrange("p (j d) -> p j d", d=D)
+            nc.vector.tensor_tensor(pair[t][:], groups[:, :, 0:2], groups[:, :, 2:4], ALU.add)
 
-        def floor_step(c, t0, t1):
-            r0, w = CHUNKS[c]
-            nc.vector.tensor_tensor(
-                work[c]["sc"][:, t0:t1, :], work[c]["sg"][:, t0:t1, :], flr_sb[:, t0:t1, r0 : r0 + w], ALU.max
-            )
+        def sum_step(t):
+            nc.vector.tensor_tensor(sum4[t][:, :], pair[t][:, :, 0], pair[t][:, :, 1], ALU.add)
 
-        def pair_step(c, t0, t1):
-            g = CHUNKS[c][1] // D
-            sc = groups(c, "sc", t0, t1)
-            nc.vector.tensor_tensor(work[c]["pair"][:, t0 * g : t1 * g, :], sc[:, :, 0:2], sc[:, :, 2:4], ALU.add)
-
-        def sum_step(c, t0, t1):
-            g = CHUNKS[c][1] // D
-            pair = work[c]["pair"][:, t0 * g : t1 * g, :]
-            nc.vector.tensor_tensor(work[c]["sum4"][:, t0 * g : t1 * g], pair[:, :, 0], pair[:, :, 1], ALU.add)
-
-        def centre_step(c, t0, t1):
-            g = CHUNKS[c][1] // D
-            sums = work[c]["sum4"][:, t0 * g : t1 * g].unsqueeze(2).to_broadcast([P, (t1 - t0) * g, D])
+        def centre_step(t, r0=0, r1=U):
+            sums = sum4[t][:, r0 // D : r1 // D].unsqueeze(2).to_broadcast([P, (r1 - r0) // D, D])
             nc.vector.scalar_tensor_tensor(
-                groups(c, "dv", t0, t1), sums, -1.0 / D, groups(c, "sc", t0, t1), ALU.mult, ALU.add
+                dv[:, t, r0:r1].rearrange("p (j d) -> p j d", d=D),
+                sums,
+                -1.0 / D,
+                sc[t][:, r0:r1].rearrange("p (j d) -> p j d", d=D),
+                ALU.mult,
+                ALU.add,
             )
 
-        def relu_step(c, t):
-            nc.vector.tensor_scalar(
-                work[c]["ru"][:, t, :], work[c]["sc"][:, t, :], 0.0, unit_sb[:, t : t + 1], ALU.max, ALU.mult
-            )
+        def relu_step(t, r0=0, r1=U):
+            nc.vector.tensor_scalar(ru[:, t, r0:r1], sc[t][:, r0:r1], 0.0, unit_sb[:, t : t + 1], ALU.max, ALU.mult)
+
+        hid = [keep.tile([P, w * PACK], BF16, name="hid%d" % r0, align_bytes=64) for r0, w in PIECES]
 
         def hidden_step(c):
+            r0, w = PIECES[c]
             nc.vector.tensor_tensor(
-                work[c]["hid"][:].rearrange("p (c i t) -> p c t i", i=2, t=PACK),
-                work[c]["dv"][:].rearrange("p t (c i) -> p c t i", i=2),
-                work[c]["ru"][:].rearrange("p t (c i) -> p c t i", i=2),
+                hid[c][:].rearrange("p (c i t) -> p c t i", i=2, t=PACK),
+                dv[:, :, r0 : r0 + w].rearrange("p t (c i) -> p c t i", i=2),
+                ru[:, :, r0 : r0 + w].rearrange("p t (c i) -> p c t i", i=2),
                 ALU.mult,
             )
 
-        def quantise(c):
-            nc.vector.quantize_mx(
-                out=work[c]["codes"][:].bitcast(FP8X4), scales=work[c]["scales"][:], in_=work[c]["hid"][:]
-            )
-
         def second_product(c):
-            r0, w = CHUNKS[c]
-            acc = psum.tile([P, w], F32, name="acc%d" % c, tag="bank%d_0" % c)
+            r0, w = PIECES[c]
+            codes = keep.tile([P, w], U32, name="codes%d" % c, align_bytes=64)
+            scales = keep.tile([P, w], U8, name="scales%d" % c, align_bytes=64)
+            nc.vector.quantize_mx(out=codes[:].bitcast(FP8X4), scales=scales[:], in_=hid[c][:])
+            acc = psum.tile([P, w], F32, name="mixed%d" % c, tag="bank%d" % (HALVES * c))
             nc.tensor.matmul_mx(
                 out=acc[:],
                 lhsT=w2_sb[:].bitcast(FP4X4),
                 lhsT_scale=w2s_sb[:],
-                rhs=work[c]["codes"][:].bitcast(FP8X4),
-                rhs_scale=work[c]["scales"][:],
+                rhs=codes[:].bitcast(FP8X4),
+                rhs_scale=scales[:],
                 start=True,
                 stop=True,
             )
-            nc.scalar.copy(work[c]["res"][:], acc[:])
-            nc.sync.dma_start(out[:, r0 : r0 + w], work[c]["res"][:])
+            res = keep.tile([P, w], F32, name="res%d" % c)
+            nc.scalar.copy(res[:], acc[:])
+            nc.sync.dma_start(out[:, r0 : r0 + w], res[:])
 
-        evacuate(0, 0)
-        evacuate(1, 0)
-        evacuate(0, 1)
-        evacuate(2, 0)
-        evacuate(1, 1)
-        fetch(0, 0)
-        fetch(0, 1)
-        evacuate(2, 1)
-        evacuate(3, 0)
-        evacuate(3, 1)
-        fetch(0, 2)
-        fetch(0, 3)
-        for c in range(1, len(CHUNKS)):
-            for t in range(PACK):
-                fetch(c, t)
+        def fetch(t):
+            nc.scalar.activation(sg[t][:, :], y[t][:].indirect(got_sb[:]), COPY)
 
-        floor_step(0, 0, 2)
-        relu_step(0, 0)
-        pair_step(0, 0, 2)
-        relu_step(0, 1)
-        sum_step(0, 0, 2)
-        floor_step(0, 2, 4)
-        centre_step(0, 0, 2)
-        pair_step(0, 2, 4)
-        relu_step(0, 2)
-        sum_step(0, 2, 4)
-        relu_step(0, 3)
-        centre_step(0, 2, 4)
-        floor_step(1, 0, 4)
+        mid = U // 2
+        for t in range(last):
+            empty_on_scalar(t, 0)
+            empty_on_vector(t, 1)
+        for h in range(HALVES):
+            for o in range(PASSES):
+                first_product(o, last, h, HALVES * h + 1)
+        for t in range(last):
+            fetch(t)
+        for h in range(HALVES):
+            empty_on_scalar(last, h)
+        fetch(last)
+
+        def relu_on_scalar(t):
+            positive = keep.tile([P, U], F32, name="positive%d" % t)
+            nc.scalar.activation(positive[:], sc[t][:], RELU)
+            nc.scalar.activation(ru[:, t, :], positive[:], COPY, scale=unit_sb[:, t : t + 1])
+
+        floor_step(0)
+        pair_step(0)
+        for t in range(1, PACK):
+            floor_step(t)
+            sum_step(t - 1)
+            pair_step(t)
+            centre_step(t - 1)
+        for t in range(2):
+            relu_on_scalar(t)
+        relu_step(last - 1)
+        sum_step(last)
+        relu_step(last)
+        centre_step(last, 0, mid)
+        centre_step(last, mid, U)
         hidden_step(0)
-        pair_step(1, 0, 4)
-        quantise(0)
-        second_product(0)
-        sum_step(1, 0, 4)
-        floor_step(2, 0, 4)
-        centre_step(1, 0, 4)
-        pair_step(2, 0, 4)
-        for t in range(PACK):
-            relu_step(1, t)
-        sum_step(2, 0, 4)
-        hidden_step(1)
-        centre_step(2, 0, 4)
-        quantise(1)
-        second_product(1)
-        for t in range(PACK):
-            relu_step(2, t)
-        hidden_step(2)
-        quantise(2)
-        second_product(2)
+        for c in range(1, len(PIECES)):
+            hidden_step(c)
+            second_product(c - 1)
+        second_product(len(PIECES) - 1)

@@ -36,43 +36,39 @@ def tile_picked_yxtrim_rect_p_kernel(
         lists = ctx.enter_context(tc.tile_pool(name="lists", bufs=1))
         keep = ctx.enter_context(tc.tile_pool(name="keep", bufs=1))
         shared = ctx.enter_context(tc.tile_pool(name="shared", bufs=1))
+        tables = ctx.enter_context(tc.tile_pool(name="tables", bufs=1))
         psum = ctx.enter_context(tc.psum_pool(name="psum", bufs=1))
 
         xs_table = shared.tile([P, T], U8, name="xs_table", align_bytes=64, offset=XS_AT)
-        nc.gpsimd.memset(xs_table[:, T // 4 : T].bitcast(I32), 0)
-        nc.vector.memset(xs_table[:, 0 : T // 4].bitcast(I32), 0)
+        nc.vector.memset(xs_table[:].bitcast(I32), 0)
         w1s_raw = shared.tile([P, PASSES, H], U8, name="w1s_raw", align_bytes=64, offset=W1S_AT)
         nc.vector.memset(w1s_raw[:].bitcast(I32), 0)
 
         offs_sb = lists.tile([P, S // PER_COL], U16, name="offs_sb")
         got_sb = lists.tile([P, U // PER_COL], U16, name="got_sb")
         nc.sync.dma_start(offs_sb[:], offs)
-        nc.sync.dma_start(got_sb[:], got)
-
-        w1_raw = keep.tile([P, PASSES, 2 * H], U8, name="w1_raw", tag="w1_then_x1", align_bytes=64)
+        w1_raw = tables.tile([P, PASSES, 2 * H], U8, name="w1_raw", align_bytes=64, offset=4 * T - 2 * H)
         nc.sync.dma_start(w1_raw[:].bitcast(I32), w1_words.rearrange("o p c -> p o c").bitcast(I32))
+        nc.sync.dma_start(got_sb[:], got)
 
         xs_rows = x_scales.rearrange("o (q j) c -> j q o c", j=4)
         for j in range(4):
             nc.sync.dma_start(xs_table[j:P:16, :].bitcast(I32), xs_rows[j].bitcast(I32))
 
-        def load_words(o, tag):
-            table = keep.tile([P, T], I32, name="xw_table%d" % o, tag=tag, align_bytes=64)
-            nc.sync.dma_start(table[:], x_words[o].rearrange("p n t -> p (n t)").bitcast(I32))
-            return table
-
-        xw_table = [load_words(0, "x0")]
-
         w1s_rows = w1_scales.rearrange("o (q j) c -> j q o c", j=4)
         for j in range(4):
-            nc.scalar.dma_start(w1s_raw[j:P:32, :, :].bitcast(I32), w1s_rows[j].bitcast(I32))
+            nc.sync.dma_start(w1s_raw[j:P:32, :, :].bitcast(I32), w1s_rows[j].bitcast(I32))
 
         w1_dealt = keep.tile([P, PASSES, PACK, 2 * P], U8, name="w1_dealt", align_bytes=64)
         w1s_dealt = shared.tile([P, PASSES, PACK, P], U8, name="w1s_dealt", align_bytes=64, offset=XS_AT)
         nc.vector.tensor_copy(
             w1_dealt[:].bitcast(U16), w1_raw[:].bitcast(U16).rearrange("p o (m t) -> p o t m", t=PACK)
         )
-        xw_table.append(load_words(1, "w1_then_x1"))
+        xw_table = []
+        for o in range(PASSES):
+            table = tables.tile([P, T], I32, name="xw_table%d" % o, align_bytes=64, offset=4 * T * o)
+            nc.sync.dma_start(table[:], x_words[o].rearrange("p n t -> p (n t)").bitcast(I32))
+            xw_table.append(table)
 
         xs_pass1 = keep.tile([P, S], U8, name="xs_pass1", align_bytes=64)
         nc.gpsimd.memset(xs_pass1[:].bitcast(I32), 0)
@@ -95,7 +91,7 @@ def tile_picked_yxtrim_rect_p_kernel(
                 xw_picked[o][:, h * HALF : (h + 1) * HALF], xw_table[o][:].bitcast(U32).indirect(offs_sb[:, cols])
             )
 
-        y = [keep.tile([P, S], F32, name="y%d" % t, align_bytes=64) for t in range(PACK)]
+        y = [keep.tile([P, S], F32, name="y%d" % t, tag="y%d" % t, align_bytes=64) for t in range(PACK)]
         banks = {}
 
         def first_product(o, t, h, bank):
@@ -220,20 +216,20 @@ def tile_picked_yxtrim_rect_p_kernel(
         fetch(last)
 
         def relu_on_scalar(t):
-            positive = keep.tile([P, U], F32, name="positive%d" % t)
+            positive = keep.tile([P, U], F32, name="positive%d" % t, tag="y%d" % last, align_bytes=64)
             nc.scalar.activation(positive[:], sc[t][:], RELU)
             nc.scalar.activation(ru[:, t, :], positive[:], COPY, scale=unit_sb[:, t : t + 1])
 
         floor_step(0)
         pair_step(0)
+        relu_step(0)
         for t in range(1, PACK):
             floor_step(t)
             sum_step(t - 1)
             pair_step(t)
             centre_step(t - 1)
-        for t in range(2):
+        for t in range(1, last):
             relu_on_scalar(t)
-        relu_step(last - 1)
         sum_step(last)
         relu_step(last)
         centre_step(last, 0, mid)

@@ -20,12 +20,24 @@ RELU = mybir.ActivationFunctionType.Relu
 P = 128
 PACK = 4
 PASSES = K // (P * PACK)
+QUAD = 32
+QUADS = P // QUAD
+ROWS = 4
+PASS1_ROW = 16
 HALF = 512
 HALVES = S // HALF
 PER_COL = 16
+RUN = 2
 PIECES = ((0, 256), (256, 128), (384, 128))
-W1S_AT = 8192
-XS_AT = W1S_AT + 1024
+
+W1S_AT = 4 * PACK * U
+FLR_AT = 64
+UNIT_AT = W1S_AT + FLR_AT
+W2_AT = UNIT_AT + 64
+W2S_AT = W2_AT + 2 * N
+XS_AT = W1S_AT + PASSES * H
+W1S_DEALT_AT = XS_AT
+XW_PICKED0_AT = XS_AT + PASSES * H
 
 
 def tile_picked_yxtrim_rect_p_kernel(
@@ -51,16 +63,16 @@ def tile_picked_yxtrim_rect_p_kernel(
         nc.sync.dma_start(w1_raw[:].bitcast(I32), w1_words.rearrange("o p c -> p o c").bitcast(I32))
         nc.sync.dma_start(got_sb[:], got)
 
-        xs_rows = x_scales.rearrange("o (q j) c -> j q o c", j=4)
-        for j in range(4):
-            nc.sync.dma_start(xs_table[j:P:16, :].bitcast(I32), xs_rows[j].bitcast(I32))
+        xs_rows = x_scales.rearrange("o (q j) c -> j q o c", j=ROWS)
+        for j in range(ROWS):
+            nc.sync.dma_start(xs_table[j:P:PASS1_ROW, :].bitcast(I32), xs_rows[j].bitcast(I32))
 
-        w1s_rows = w1_scales.rearrange("o (q j) c -> j q o c", j=4)
-        for j in range(4):
-            nc.sync.dma_start(w1s_raw[j:P:32, :, :].bitcast(I32), w1s_rows[j].bitcast(I32))
+        w1s_rows = w1_scales.rearrange("o (q j) c -> j q o c", j=ROWS)
+        for j in range(ROWS):
+            nc.sync.dma_start(w1s_raw[j:P:QUAD, :, :].bitcast(I32), w1s_rows[j].bitcast(I32))
 
         w1_dealt = keep.tile([P, PASSES, PACK, 2 * P], U8, name="w1_dealt", align_bytes=64)
-        w1s_dealt = shared.tile([P, PASSES, PACK, P], U8, name="w1s_dealt", align_bytes=64, offset=XS_AT)
+        w1s_dealt = shared.tile([P, PASSES, PACK, P], U8, name="w1s_dealt", align_bytes=64, offset=W1S_DEALT_AT)
         nc.vector.tensor_copy(
             w1_dealt[:].bitcast(U16), w1_raw[:].bitcast(U16).rearrange("p o (m t) -> p o t m", t=PACK)
         )
@@ -74,25 +86,30 @@ def tile_picked_yxtrim_rect_p_kernel(
         nc.gpsimd.memset(xs_pass1[:].bitcast(I32), 0)
         xs_picked = keep.tile([P, S], U8, name="xs_picked", align_bytes=64)
         nc.vector.tensor_copy(xs_picked[:], xs_table[:].indirect(offs_sb[:]))
-        for q in range(4):
+        for q in range(QUADS):
+            row = QUAD * q
             nc.scalar.dma_start(
-                xs_pass1[32 * q : 32 * q + 4, :].bitcast(I32), xs_picked[32 * q + 16 : 32 * q + 20, :].bitcast(I32)
+                xs_pass1[row : row + ROWS, :].bitcast(I32),
+                xs_picked[row + PASS1_ROW : row + PASS1_ROW + ROWS, :].bitcast(I32),
             )
         xs_planes = (xs_picked, xs_pass1)
 
         xw_picked = [
-            shared.tile([P, S], U32, name="xw_picked0", align_bytes=64, offset=XS_AT + 1024),
+            shared.tile([P, S], U32, name="xw_picked0", align_bytes=64, offset=XW_PICKED0_AT),
             keep.tile([P, S], U32, name="xw_picked1", align_bytes=64),
         ]
 
         def pick(o, h):
-            cols = slice(h * HALF // PER_COL, (h + 1) * HALF // PER_COL)
+            entries = slice(h * HALF // PER_COL, (h + 1) * HALF // PER_COL)
             nc.vector.tensor_copy(
-                xw_picked[o][:, h * HALF : (h + 1) * HALF], xw_table[o][:].bitcast(U32).indirect(offs_sb[:, cols])
+                xw_picked[o][:, h * HALF : (h + 1) * HALF], xw_table[o][:].bitcast(U32).indirect(offs_sb[:, entries])
             )
 
         y = [keep.tile([P, S], F32, name="y%d" % t, tag="y%d" % t, align_bytes=64) for t in range(PACK)]
         banks = {}
+
+        def bank_of(t, h):
+            return HALVES * t + h
 
         def first_product(o, t, h, bank):
             cols = slice(h * HALF, (h + 1) * HALF)
@@ -118,17 +135,18 @@ def tile_picked_yxtrim_rect_p_kernel(
         pick(0, 0)
         nc.vector.tensor_copy(w1s_dealt[:], w1s_raw[:].rearrange("p o (m t) -> p o t m", t=PACK))
 
-        flr_sb = shared.tile([P, PACK, U], F32, name="flr_sb", offset=64)
+        flr_sb = shared.tile([P, PACK, U], F32, name="flr_sb", offset=FLR_AT)
         nc.sync.dma_start(flr_sb[:], flr.rearrange("(p t) r -> p t r", t=PACK))
-        unit_sb = shared.tile([P, PACK], F32, name="unit_sb", offset=W1S_AT + 64)
+        unit_sb = shared.tile([P, PACK], F32, name="unit_sb", offset=UNIT_AT)
         nc.sync.dma_start(unit_sb[:], unit.rearrange("(p t) o -> p (t o)", t=PACK))
-        w2_sb = shared.tile([P, 2 * N], U8, name="w2_sb", align_bytes=64, offset=W1S_AT + 128)
+        w2_sb = shared.tile([P, 2 * N], U8, name="w2_sb", align_bytes=64, offset=W2_AT)
         nc.sync.dma_start(w2_sb[:].bitcast(I32), w2_words[0].bitcast(I32))
-        w2s_sb = shared.tile([P, N], U8, name="w2s_sb", align_bytes=64, offset=W1S_AT + 384)
+        w2s_sb = shared.tile([P, N], U8, name="w2s_sb", align_bytes=64, offset=W2S_AT)
         nc.gpsimd.memset(w2s_sb[:].bitcast(I32), 0)
-        for q in range(4):
+        for q in range(QUADS):
             nc.sync.dma_start(
-                w2s_sb[32 * q : 32 * q + 4, :].bitcast(I32), w2_scales[0, 4 * q : 4 * q + 4, :].bitcast(I32)
+                w2s_sb[QUAD * q : QUAD * q + ROWS, :].bitcast(I32),
+                w2_scales[0, ROWS * q : ROWS * (q + 1), :].bitcast(I32),
             )
 
         for o in range(PASSES):
@@ -136,7 +154,7 @@ def tile_picked_yxtrim_rect_p_kernel(
                 if (o, h) != (0, 0):
                     pick(o, h)
                 for t in range(last):
-                    first_product(o, t, h, HALVES * t + h)
+                    first_product(o, t, h, bank_of(t, h))
 
         sg = [keep.tile([P, U], F32, name="sg%d" % t) for t in range(PACK)]
         sc = [keep.tile([P, U], F32, name="sc%d" % t) for t in range(PACK)]
@@ -145,15 +163,15 @@ def tile_picked_yxtrim_rect_p_kernel(
         dv = keep.tile([P, PACK, U], F32, name="dv")
         ru = keep.tile([P, PACK, U], F32, name="ru")
 
-        def floor_step(t, r0=0, r1=U):
-            nc.vector.tensor_tensor(sc[t][:, r0:r1], sg[t][:, r0:r1], flr_sb[:, t, r0:r1], ALU.max)
+        def floor_step(t):
+            nc.vector.tensor_tensor(sc[t][:], sg[t][:], flr_sb[:, t, :], ALU.max)
 
         def pair_step(t):
-            groups = sc[t][:, :].rearrange("p (j d) -> p j d", d=D)
+            groups = sc[t][:].rearrange("p (j d) -> p j d", d=D)
             nc.vector.tensor_tensor(pair[t][:], groups[:, :, 0:2], groups[:, :, 2:4], ALU.add)
 
         def sum_step(t):
-            nc.vector.tensor_tensor(sum4[t][:, :], pair[t][:, :, 0], pair[t][:, :, 1], ALU.add)
+            nc.vector.tensor_tensor(sum4[t][:], pair[t][:, :, 0], pair[t][:, :, 1], ALU.add)
 
         def centre_step(t, r0=0, r1=U):
             sums = sum4[t][:, r0 // D : r1 // D].unsqueeze(2).to_broadcast([P, (r1 - r0) // D, D])
@@ -166,17 +184,17 @@ def tile_picked_yxtrim_rect_p_kernel(
                 ALU.add,
             )
 
-        def relu_step(t, r0=0, r1=U):
-            nc.vector.tensor_scalar(ru[:, t, r0:r1], sc[t][:, r0:r1], 0.0, unit_sb[:, t : t + 1], ALU.max, ALU.mult)
+        def relu_on_vector(t):
+            nc.vector.tensor_scalar(ru[:, t, :], sc[t][:], 0.0, unit_sb[:, t : t + 1], ALU.max, ALU.mult)
 
         hid = [keep.tile([P, w * PACK], BF16, name="hid%d" % r0, align_bytes=64) for r0, w in PIECES]
 
         def hidden_step(c):
             r0, w = PIECES[c]
             nc.vector.tensor_tensor(
-                hid[c][:].rearrange("p (c i t) -> p c t i", i=2, t=PACK),
-                dv[:, :, r0 : r0 + w].rearrange("p t (c i) -> p c t i", i=2),
-                ru[:, :, r0 : r0 + w].rearrange("p t (c i) -> p c t i", i=2),
+                hid[c][:].rearrange("p (g i t) -> p g t i", i=RUN, t=PACK),
+                dv[:, :, r0 : r0 + w].rearrange("p t (g i) -> p g t i", i=RUN),
+                ru[:, :, r0 : r0 + w].rearrange("p t (g i) -> p g t i", i=RUN),
                 ALU.mult,
             )
 
@@ -185,7 +203,7 @@ def tile_picked_yxtrim_rect_p_kernel(
             codes = keep.tile([P, w], U32, name="codes%d" % c, align_bytes=64)
             scales = keep.tile([P, w], U8, name="scales%d" % c, align_bytes=64)
             nc.vector.quantize_mx(out=codes[:].bitcast(FP8X4), scales=scales[:], in_=hid[c][:])
-            acc = psum.tile([P, w], F32, name="mixed%d" % c, tag="bank%d" % (HALVES * c))
+            acc = psum.tile([P, w], F32, name="mixed%d" % c, tag="bank%d" % bank_of(c, 0))
             nc.tensor.matmul_mx(
                 out=acc[:],
                 lhsT=w2_sb[:].bitcast(FP4X4),
@@ -200,15 +218,16 @@ def tile_picked_yxtrim_rect_p_kernel(
             nc.sync.dma_start(out[:, r0 : r0 + w], res[:])
 
         def fetch(t):
-            nc.scalar.activation(sg[t][:, :], y[t][:].indirect(got_sb[:]), COPY)
+            nc.scalar.activation(sg[t][:], y[t][:].indirect(got_sb[:]), COPY)
 
-        mid = U // 2
-        for t in range(last):
+        for t in range(last - 1):
             empty_on_scalar(t, 0)
             empty_on_vector(t, 1)
         for h in range(HALVES):
+            empty_on_vector(last - 1, h)
+        for h in range(HALVES):
             for o in range(PASSES):
-                first_product(o, last, h, HALVES * h + 1)
+                first_product(o, last, h, bank_of(last - 1, h))
         for t in range(last):
             fetch(t)
         for h in range(HALVES):
@@ -222,7 +241,7 @@ def tile_picked_yxtrim_rect_p_kernel(
 
         floor_step(0)
         pair_step(0)
-        relu_step(0)
+        relu_on_vector(0)
         for t in range(1, PACK):
             floor_step(t)
             sum_step(t - 1)
@@ -231,9 +250,10 @@ def tile_picked_yxtrim_rect_p_kernel(
         for t in range(1, last):
             relu_on_scalar(t)
         sum_step(last)
-        relu_step(last)
-        centre_step(last, 0, mid)
-        centre_step(last, mid, U)
+        relu_on_vector(last)
+        first_width = PIECES[0][1]
+        centre_step(last, 0, first_width)
+        centre_step(last, first_width, U)
         hidden_step(0)
         for c in range(1, len(PIECES)):
             hidden_step(c)

from contextlib import ExitStack

import concourse.mybir as mybir

K, T, S, D, N, H, U = 1024, 2048, 1024, 4, 128, 512, 512
FLOPS = 2 * K * H * S + 2 * H * N * U

F32 = mybir.dt.float32
BF16 = mybir.dt.bfloat16
I32 = mybir.dt.int32
U32 = mybir.dt.uint32
U16 = mybir.dt.uint16
U8 = mybir.dt.uint8
FP8X4 = mybir.dt.float8_e4m3fn_x4
FP4X4 = mybir.dt.float4_e2m1fn_x4
ALU = mybir.AluOpType
COPY = mybir.ActivationFunctionType.Copy
RELU = mybir.ActivationFunctionType.Relu

P = 128
PACK = 4
PASSES = K // (P * PACK)
QUAD = 32
QUADS = P // QUAD
ROWS = 4
PASS1_ROW = 16
HALF = 512
HALVES = S // HALF
PER_COL = 16
RUN = 2
PIECES = ((0, 256), (256, 128), (384, 128))

W1S_AT = 4 * PACK * U
FLR_AT = 64
UNIT_AT = W1S_AT + FLR_AT
W2_AT = UNIT_AT + 64
W2S_AT = W2_AT + 2 * N
XS_AT = W1S_AT + PASSES * H
W1S_DEALT_AT = XS_AT
XW_PICKED0_AT = XS_AT + PASSES * H


def tile_picked_yxtrim_rect_p_kernel(
    tc, x_words, x_scales, w1_words, w1_scales, flr, unit, w2_words, w2_scales, offs, got, out
):
    nc = tc.nc
    with ExitStack() as ctx:
        lists = ctx.enter_context(tc.tile_pool(name="lists", bufs=1))
        keep = ctx.enter_context(tc.tile_pool(name="keep", bufs=1))
        shared = ctx.enter_context(tc.tile_pool(name="shared", bufs=1))
        tables = ctx.enter_context(tc.tile_pool(name="tables", bufs=1))
        psum = ctx.enter_context(tc.psum_pool(name="psum", bufs=1))

        xs_table = shared.tile([P, T], U8, name="xs_table", align_bytes=64, offset=XS_AT)
        nc.vector.memset(xs_table[:].bitcast(I32), 0)
        w1s_raw = shared.tile([P, PASSES, H], U8, name="w1s_raw", align_bytes=64, offset=W1S_AT)
        nc.vector.memset(w1s_raw[:].bitcast(I32), 0)

        offs_sb = lists.tile([P, S // PER_COL], U16, name="offs_sb")
        got_sb = lists.tile([P, U // PER_COL], U16, name="got_sb")
        nc.sync.dma_start(offs_sb[:], offs)
        w1_raw = tables.tile([P, PASSES, 2 * H], U8, name="w1_raw", align_bytes=64, offset=4 * T - 2 * H)
        nc.sync.dma_start(w1_raw[:].bitcast(I32), w1_words.rearrange("o p c -> p o c").bitcast(I32))
        nc.sync.dma_start(got_sb[:], got)

        xs_rows = x_scales.rearrange("o (q j) c -> j q o c", j=ROWS)
        for j in range(ROWS):
            nc.sync.dma_start(xs_table[j:P:PASS1_ROW, :].bitcast(I32), xs_rows[j].bitcast(I32))

        w1s_rows = w1_scales.rearrange("o (q j) c -> j q o c", j=ROWS)
        for j in range(ROWS):
            nc.sync.dma_start(w1s_raw[j:P:QUAD, :, :].bitcast(I32), w1s_rows[j].bitcast(I32))

        w1_dealt = keep.tile([P, PASSES, PACK, 2 * P], U8, name="w1_dealt", align_bytes=64)
        w1s_dealt = shared.tile([P, PASSES, PACK, P], U8, name="w1s_dealt", align_bytes=64, offset=W1S_DEALT_AT)
        nc.vector.tensor_copy(
            w1_dealt[:].bitcast(U16), w1_raw[:].bitcast(U16).rearrange("p o (m t) -> p o t m", t=PACK)
        )
        xw_table = []
        for o in range(PASSES):
            table = tables.tile([P, T], I32, name="xw_table%d" % o, align_bytes=64, offset=4 * T * o)
            nc.sync.dma_start(table[:], x_words[o].rearrange("p n t -> p (n t)").bitcast(I32))
            xw_table.append(table)

        xs_pass1 = keep.tile([P, S], U8, name="xs_pass1", align_bytes=64)
        nc.gpsimd.memset(xs_pass1[:].bitcast(I32), 0)
        xs_picked = keep.tile([P, S], U8, name="xs_picked", align_bytes=64)
        nc.vector.tensor_copy(xs_picked[:], xs_table[:].indirect(offs_sb[:]))
        for q in range(QUADS):
            row = QUAD * q
            nc.scalar.dma_start(
                xs_pass1[row : row + ROWS, :].bitcast(I32),
                xs_picked[row + PASS1_ROW : row + PASS1_ROW + ROWS, :].bitcast(I32),
            )
        xs_planes = (xs_picked, xs_pass1)

        xw_picked = [
            shared.tile([P, S], U32, name="xw_picked0", align_bytes=64, offset=XW_PICKED0_AT),
            keep.tile([P, S], U32, name="xw_picked1", align_bytes=64),
        ]

        def pick(o, h):
            entries = slice(h * HALF // PER_COL, (h + 1) * HALF // PER_COL)
            nc.vector.tensor_copy(
                xw_picked[o][:, h * HALF : (h + 1) * HALF], xw_table[o][:].bitcast(U32).indirect(offs_sb[:, entries])
            )

        y = [keep.tile([P, S], F32, name="y%d" % t, tag="y%d" % t, align_bytes=64) for t in range(PACK)]
        banks = {}

        def bank_of(t, h):
            return HALVES * t + h

        def first_product(o, t, h, bank):
            cols = slice(h * HALF, (h + 1) * HALF)
            if o == 0:
                banks[t, h] = psum.tile([P, HALF], F32, name="acc%d_%d" % (t, h), tag="bank%d" % bank)
            nc.tensor.matmul_mx(
                out=banks[t, h][:],
                lhsT=w1_dealt[:, o, t, :].bitcast(FP4X4),
                lhsT_scale=w1s_dealt[:, o, t, :],
                rhs=xw_picked[o][:, cols].bitcast(FP8X4),
                rhs_scale=xs_planes[o][:, cols],
                start=(o == 0),
                stop=(o == PASSES - 1),
            )

        def empty_on_scalar(t, h):
            nc.scalar.copy(y[t][:, h * HALF : (h + 1) * HALF], banks[t, h][:])

        def empty_on_vector(t, h):
            nc.vector.tensor_copy(y[t][:, h * HALF : (h + 1) * HALF], banks[t, h][:])

        last = PACK - 1
        pick(0, 0)
        nc.vector.tensor_copy(w1s_dealt[:], w1s_raw[:].rearrange("p o (m t) -> p o t m", t=PACK))

        flr_sb = shared.tile([P, PACK, U], F32, name="flr_sb", offset=FLR_AT)
        nc.sync.dma_start(flr_sb[:], flr.rearrange("(p t) r -> p t r", t=PACK))
        unit_sb = shared.tile([P, PACK], F32, name="unit_sb", offset=UNIT_AT)
        nc.sync.dma_start(unit_sb[:], unit.rearrange("(p t) o -> p (t o)", t=PACK))
        w2_sb = shared.tile([P, 2 * N], U8, name="w2_sb", align_bytes=64, offset=W2_AT)
        nc.sync.dma_start(w2_sb[:].bitcast(I32), w2_words[0].bitcast(I32))
        w2s_sb = shared.tile([P, N], U8, name="w2s_sb", align_bytes=64, offset=W2S_AT)
        nc.gpsimd.memset(w2s_sb[:].bitcast(I32), 0)
        for q in range(QUADS):
            nc.sync.dma_start(
                w2s_sb[QUAD * q : QUAD * q + ROWS, :].bitcast(I32),
                w2_scales[0, ROWS * q : ROWS * (q + 1), :].bitcast(I32),
            )

        for o in range(PASSES):
            for h in range(HALVES):
                if (o, h) != (0, 0):
                    pick(o, h)
                for t in range(last):
                    first_product(o, t, h, bank_of(t, h))

        sg = [keep.tile([P, U], F32, name="sg%d" % t) for t in range(PACK)]
        sc = [keep.tile([P, U], F32, name="sc%d" % t) for t in range(PACK)]
        pair = [keep.tile([P, U // D, 2], F32, name="pair%d" % t) for t in range(PACK)]
        sum4 = [keep.tile([P, U // D], F32, name="sum4_%d" % t) for t in range(PACK)]
        dv = keep.tile([P, PACK, U], F32, name="dv")
        ru = keep.tile([P, PACK, U], F32, name="ru")

        def floor_step(t):
            nc.vector.tensor_tensor(sc[t][:], sg[t][:], flr_sb[:, t, :], ALU.max)

        def pair_step(t):
            groups = sc[t][:].rearrange("p (j d) -> p j d", d=D)
            nc.vector.tensor_tensor(pair[t][:], groups[:, :, 0:2], groups[:, :, 2:4], ALU.add)

        def sum_step(t):
            nc.vector.tensor_tensor(sum4[t][:], pair[t][:, :, 0], pair[t][:, :, 1], ALU.add)

        def centre_step(t, r0=0, r1=U):
            sums = sum4[t][:, r0 // D : r1 // D].unsqueeze(2).to_broadcast([P, (r1 - r0) // D, D])
            nc.vector.scalar_tensor_tensor(
                dv[:, t, r0:r1].rearrange("p (j d) -> p j d", d=D),
                sums,
                -1.0 / D,
                sc[t][:, r0:r1].rearrange("p (j d) -> p j d", d=D),
                ALU.mult,
                ALU.add,
            )

        def relu_on_vector(t):
            nc.vector.tensor_scalar(ru[:, t, :], sc[t][:], 0.0, unit_sb[:, t : t + 1], ALU.max, ALU.mult)

        hid = [keep.tile([P, w * PACK], BF16, name="hid%d" % r0, align_bytes=64) for r0, w in PIECES]

        def hidden_step(c):
            r0, w = PIECES[c]
            nc.vector.tensor_tensor(
                hid[c][:].rearrange("p (g i t) -> p g t i", i=RUN, t=PACK),
                dv[:, :, r0 : r0 + w].rearrange("p t (g i) -> p g t i", i=RUN),
                ru[:, :, r0 : r0 + w].rearrange("p t (g i) -> p g t i", i=RUN),
                ALU.mult,
            )

        def second_product(c):
            r0, w = PIECES[c]
            codes = keep.tile([P, w], U32, name="codes%d" % c, align_bytes=64)
            scales = keep.tile([P, w], U8, name="scales%d" % c, align_bytes=64)
            nc.vector.quantize_mx(out=codes[:].bitcast(FP8X4), scales=scales[:], in_=hid[c][:])
            acc = psum.tile([P, w], F32, name="mixed%d" % c, tag="bank%d" % bank_of(c, 0))
            nc.tensor.matmul_mx(
                out=acc[:],
                lhsT=w2_sb[:].bitcast(FP4X4),
                lhsT_scale=w2s_sb[:],
                rhs=codes[:].bitcast(FP8X4),
                rhs_scale=scales[:],
                start=True,
                stop=True,
            )
            res = keep.tile([P, w], F32, name="res%d" % c)
            nc.scalar.copy(res[:], acc[:])
            nc.sync.dma_start(out[:, r0 : r0 + w], res[:])

        def fetch(t):
            nc.scalar.activation(sg[t][:], y[t][:].indirect(got_sb[:]), COPY)

        for t in range(last - 1):
            empty_on_scalar(t, 0)
            empty_on_vector(t, 1)
        for h in range(HALVES):
            empty_on_vector(last - 1, h)
        for h in range(HALVES):
            for o in range(PASSES):
                first_product(o, last, h, bank_of(last - 1, h))
        for t in range(last):
            fetch(t)
        for h in range(HALVES):
            empty_on_scalar(last, h)
        fetch(last)

        def relu_on_scalar(t):
            positive = keep.tile([P, U], F32, name="positive%d" % t, tag="y%d" % last, align_bytes=64)
            nc.scalar.activation(positive[:], sc[t][:], RELU)
            nc.scalar.activation(ru[:, t, :], positive[:], COPY, scale=unit_sb[:, t : t + 1])

        floor_step(0)
        pair_step(0)
        relu_on_vector(0)
        for t in range(1, PACK):
            floor_step(t)
            sum_step(t - 1)
            pair_step(t)
            centre_step(t - 1)
        for t in range(1, last):
            relu_on_scalar(t)
        sum_step(last)
        relu_on_vector(last)
        first_width = PIECES[0][1]
        centre_step(last, 0, first_width)
        centre_step(last, first_width, U)
        hidden_step(0)
        for c in range(1, len(PIECES)):
            hidden_step(c)
            second_product(c - 1)
        second_product(len(PIECES) - 1)
